import numpy as np
import ml_dtypes


def mxq(x, axis, fmt="e4m3"):
    dtype, down = {"e4m3": (ml_dtypes.float8_e4m3fn, 7), "e5m2": (ml_dtypes.float8_e5m2, 14)}[fmt]
    v = np.moveaxis(np.asarray(x, np.float32).astype(ml_dtypes.bfloat16).astype(np.float64), axis, -1)
    blocks = v.reshape(v.shape[:-1] + (-1, 32))
    amax = np.abs(blocks).max(-1, keepdims=True)
    byte = np.maximum(np.where(amax > 0, np.frexp(amax)[1] - 1 + 127, 0) - down, 1)
    scale = np.exp2(byte - 127.0)
    codes = (blocks / scale).astype(np.float32).astype(dtype).astype(np.float64)
    return np.moveaxis((codes * scale).reshape(v.shape), -1, axis)


WIDE = False


def mx_kscale(k):
    if not WIDE:
        return np.ones(k)
    levels = np.array([10, -10, 5, -5, 0])
    if k % 512:
        return np.exp2(np.random.permutation(np.resize(levels, k // 32))).repeat(32)
    a = np.empty((k // 512, 16))
    for p in range(k // 512):
        a[p, :8] = np.random.permutation(np.resize(levels, 8))
        for g in range(8):
            far = levels[np.abs(levels - a[p, g]) >= 10]
            a[p, g + 8] = far[np.random.randint(len(far))]
    return np.exp2(a.ravel()).repeat(32)


def f64(x):
    return np.asarray(x).astype(np.float64)


E2M1 = np.array([0.0, 0.5, 1.0, 1.5, 2.0, 3.0, 4.0, 6.0, -0.0, -0.5, -1.0, -1.5, -2.0, -3.0, -4.0, -6.0])


def pack_weight(w, fmt):
    k, n = w.shape
    w = f64(np.asarray(w, np.float32).astype(ml_dtypes.bfloat16)).reshape(k // 32, 32, n)
    amax = np.abs(w).max(1)
    if fmt == "e4m3":
        byte = np.frexp(amax)[1] - 1 + 127 - 7
    else:
        mant, ex = np.frexp(amax / 6.0)
        byte = np.where(mant > 0.5, ex, ex - 1) + 127
    byte = np.clip(np.where(amax > 0, byte, 1), 1, 254)
    scaled = (w * np.exp2(127.0 - byte)[:, None, :]).reshape(k, n).astype(np.float32)
    by_word = np.ascontiguousarray(scaled.reshape(k // 512, 128, 4, n).transpose(0, 1, 3, 2))
    if fmt == "e4m3":
        words = by_word.astype(ml_dtypes.float8_e4m3fn).view(np.uint8)
    else:
        c = by_word.astype(ml_dtypes.float4_e2m1fn).view(np.uint8) & 0xF
        words = (c[..., 0::2] | (c[..., 1::2] << 4)).reshape(k // 512, 128, 2 * n)
    return np.ascontiguousarray(words), np.ascontiguousarray(byte.astype(np.uint8).reshape(k // 512, 16, n))


def unpack_weight(words, scales, fmt):
    g, _, n = scales.shape
    words = np.ascontiguousarray(words).reshape(g, 128, n, -1)
    if fmt == "e4m3":
        vals = words.view(ml_dtypes.float8_e4m3fn).astype(np.float64)
    else:
        nib = np.empty((g, 128, n, 4), np.uint8)
        nib[..., 0::2] = words & 0xF
        nib[..., 1::2] = words >> 4
        vals = E2M1[nib]
    vals = vals * np.repeat(np.exp2(scales.astype(np.float64) - 127.0), 8, axis=1)[..., None]
    return vals.transpose(0, 1, 3, 2).reshape(g * 512, n)


K, Q, V, T = 1536, 1024, 512, 512


def setup_inputs():
    n = np.random.standard_normal
    s = mx_kscale(K)[:, None]
    p_wq = pack_weight(n((K, Q)) / np.sqrt(K) / s, "e2m1")
    p_wk = pack_weight(n((K, V)) / np.sqrt(K) / s, "e4m3")
    return {
        "x": (n((K, T)) * s).astype(np.float32),
        "wq_words": p_wq[0],
        "wq_scales": p_wq[1],
        "wk_words": p_wk[0],
        "wk_scales": p_wk[1],
        "wv": (n((K, V)) / np.sqrt(K) / s).astype(np.float32),
    }


def reference(x, wq_words, wq_scales, wk_words, wk_scales, wv):
    x_ = mxq(f64(x), 0, "e4m3")
    wq_ = unpack_weight(wq_words, wq_scales, "e2m1")
    wk_ = unpack_weight(wk_words, wk_scales, "e4m3")
    wv_ = mxq(f64(wv), 0, "e4m3")
    return x_.T @ wq_, x_.T @ wk_, x_.T @ wv_

@@ -1,0 +1,151 @@
+from contextlib import ExitStack
+
+import concourse.mybir as mybir
+
+K, Q, V, T = 1536, 1024, 512, 512
+FLOPS = 2 * K * T * (Q + 2 * V)
+
+F32 = mybir.dt.float32
+BF16 = mybir.dt.bfloat16
+I32 = mybir.dt.int32
+U32 = mybir.dt.uint32
+U8 = mybir.dt.uint8
+E4M3X4 = mybir.dt.float8_e4m3fn_x4
+E2M1X4 = mybir.dt.float4_e2m1fn_x4
+
+P = 128
+PACK = 4
+K_PASS = P * PACK
+PASSES = K // K_PASS
+ROWS = T // P
+N_MM = 512
+
+CAST_SPLIT = 384
+
+
+def tile_mix_qkv3_tm_none_kernel(
+    tc, x, wq_words, wq_scales, wk_words, wk_scales, wv, out_0, out_1, out_2
+):
+    nc = tc.nc
+    with ExitStack() as ctx:
+        sb = ctx.enter_context(tc.tile_pool(name="sb", bufs=1))
+        psum = ctx.enter_context(tc.psum_pool(name="psum", bufs=1))
+
+        x_raw = [sb.tile([P, PACK, T], F32, name=f"x_raw{a}", align_bytes=64) for a in range(PASSES)]
+        wv_raw = [sb.tile([P, PACK, V], F32, name=f"wv_raw{a}", align_bytes=64) for a in range(PASSES)]
+        x_grp = [sb.tile([P, ROWS, P, PACK], BF16, name=f"x_grp{a}", align_bytes=64) for a in range(PASSES)]
+        wv_grp = [sb.tile([P, V, PACK], BF16, name=f"wv_grp{a}", align_bytes=64) for a in range(PASSES)]
+        x_codes = [sb.tile([P, T], U32, name=f"x_codes{a}", align_bytes=64) for a in range(PASSES)]
+        x_sc = [sb.tile([P, T], U8, name=f"x_sc{a}", align_bytes=64) for a in range(PASSES)]
+        wv_codes = [sb.tile([P, V], U32, name=f"wv_codes{a}", align_bytes=64) for a in range(PASSES)]
+        wv_sc = [sb.tile([P, V], U8, name=f"wv_sc{a}", align_bytes=64) for a in range(PASSES)]
+        wq_sb = sb.tile([P, PASSES, 2 * Q], U8, name="wq_sb", align_bytes=64)
+        wk_sb = sb.tile([P, PASSES, PACK * V], U8, name="wk_sb", align_bytes=64)
+        wq_sc = sb.tile([P, PASSES, Q], U8, name="wq_sc", align_bytes=64)
+        wk_sc = sb.tile([P, PASSES, V], U8, name="wk_sc", align_bytes=64)
+        q_out = sb.tile([P, ROWS, Q], F32, name="q_out", align_bytes=64)
+        k_out = sb.tile([P, ROWS, V], F32, name="k_out", align_bytes=64)
+        v_out = sb.tile([P, ROWS, V], F32, name="v_out", align_bytes=64)
+
+        def load_pass(dst, src, a):
+            rows = src[a * K_PASS : (a + 1) * K_PASS, :]
+            nc.sync.dma_start(out=dst[:], in_=rows.rearrange("(p j) w -> p j w", j=PACK))
+
+        def load_scales(dst, src):
+            words = src.bitcast(I32).rearrange("a (q r) n -> r q a n", r=4)
+            for r in range(4):
+                nc.sync.dma_start(out=dst[r:P:32, :, :].bitcast(I32), in_=words[r])
+
+        def cast_x(a):
+            dst = x_grp[a][:].rearrange("p i m j -> p m j i")
+            src = x_raw[a][:].rearrange("p j (m i) -> p m j i", i=ROWS)
+            s = CAST_SPLIT // ROWS
+            nc.vector.tensor_copy(out=dst[:, :s], in_=src[:, :s])
+            nc.scalar.copy(out=dst[:, s:], in_=src[:, s:])
+
+        def cast_wv(a):
+            dst = wv_grp[a][:].rearrange("p (c i) j -> p c j i", i=4)
+            src = wv_raw[a][:].rearrange("p j (c i) -> p c j i", i=4)
+            s = CAST_SPLIT // 4
+            nc.vector.tensor_copy(out=dst[:, :s], in_=src[:, :s])
+            nc.scalar.copy(out=dst[:, s:], in_=src[:, s:])
+
+        def x_operand(a, i):
+            cols = slice(i * P, (i + 1) * P)
+            return x_codes[a][:, cols].bitcast(E4M3X4), x_sc[a][:, cols]
+
+        def multiply(acc, a, i, rhs, rhs_scale):
+            lhsT, lhsT_scale = x_operand(a, i)
+            nc.tensor.matmul_mx(
+                out=acc[:], lhsT=lhsT, lhsT_scale=lhsT_scale, rhs=rhs, rhs_scale=rhs_scale,
+                start=(a == 0), stop=(a == PASSES - 1),
+            )
+
+        def store_rows(out, tile, i):
+            rows = out.rearrange("(m i) n -> m i n", i=ROWS)
+            nc.sync.dma_start(out=rows[:, i : i + 2, :], in_=tile[:, i : i + 2, :])
+
+        def multiply_v(acc, a, i):
+            multiply(acc, a, i, wv_codes[a][:].bitcast(E4M3X4), wv_sc[a][:])
+
+        with tc.manual_schedule():
+            nc.vector.memset(wq_sc[:].bitcast(I32), 0)
+            nc.vector.memset(wk_sc[:].bitcast(I32), 0)
+            load_pass(x_raw[0], x, 0)
+            load_scales(wq_sc, wq_scales)
+            nc.sync.dma_start(out=wq_sb[:, 0, :], in_=wq_words[0])
+            for a in range(1, PASSES):
+                load_pass(x_raw[a], x, a)
+                nc.sync.dma_start(out=wq_sb[:, a, :], in_=wq_words[a])
+            load_scales(wk_sc, wk_scales)
+            nc.sync.dma_start(out=wk_sb[:], in_=wk_words.rearrange("a p m i -> p a (m i)"))
+            for a in range(PASSES):
+                load_pass(wv_raw[a], wv, a)
+
+            q_acc = [psum.tile([P, N_MM], F32, name=f"bank{b}") for b in range(8)]
+            for a in range(PASSES):
+                cast_x(a)
+                nc.vector.quantize_mx(
+                    out=x_codes[a][:].bitcast(E4M3X4), scales=x_sc[a][:],
+                    in_=x_grp[a][:].rearrange("p i m j -> p (i m j)"),
+                )
+                for i in range(ROWS):
+                    for h in range(2):
+                        n = slice(h * N_MM, (h + 1) * N_MM)
+                        multiply(
+                            q_acc[2 * i + h], a, i,
+                            wq_sb[:, a, 2 * h * N_MM : 2 * (h + 1) * N_MM].bitcast(E2M1X4),
+                            wq_sc[:, a, n],
+                        )
+            for i in range(ROWS):
+                nc.vector.tensor_copy(out=q_out[:, i, :N_MM], in_=q_acc[2 * i][:])
+                nc.scalar.copy(out=q_out[:, i, N_MM:], in_=q_acc[2 * i + 1][:])
+                if i % 2 == 1:
+                    store_rows(out_0, q_out, i - 1)
+
+            k_acc = [psum.tile([P, N_MM], F32, name=f"bank{b}") for b in range(4)]
+            for i in range(ROWS):
+                for a in range(PASSES):
+                    multiply(k_acc[i], a, i, wk_sb[:, a, :].bitcast(E4M3X4), wk_sc[:, a, :])
+
+            def quantize_wv(a):
+                nc.vector.quantize_mx(
+                    out=wv_codes[a][:].bitcast(E4M3X4), scales=wv_sc[a][:],
+                    in_=wv_grp[a][:].rearrange("p w j -> p (w j)"),
+                )
+
+            v_acc = [psum.tile([P, N_MM], F32, name=f"bank{b}") for b in range(4, 8)]
+            for a in range(PASSES):
+                cast_wv(a)
+                quantize_wv(a)
+                for i in range(ROWS):
+                    multiply_v(v_acc[i], a, i)
+                if a < 2:
+                    nc.vector.tensor_copy(out=k_out[:, 2 * a, :], in_=k_acc[2 * a][:])
+                    nc.scalar.copy(out=k_out[:, 2 * a + 1, :], in_=k_acc[2 * a + 1][:])
+            nc.sync.dma_start(out=out_1.rearrange("(m i) n -> m i n", i=ROWS), in_=k_out[:])
+
+            for i in range(0, ROWS, 2):
+                nc.vector.tensor_copy(out=v_out[:, i, :], in_=v_acc[i][:])
+                nc.scalar.copy(out=v_out[:, i + 1, :], in_=v_acc[i + 1][:])
+                store_rows(out_2, v_out, i)

@@ -20,7 +20,7 @@ PASSES = K // K_PASS
 ROWS = T // P
 N_MM = 512
 
-CAST_SPLIT = 384
+CAST_SPLIT = 352
 
 
 def tile_mix_qkv3_tm_none_kernel(
@@ -81,9 +81,8 @@ def tile_mix_qkv3_tm_none_kernel(
                 start=(a == 0), stop=(a == PASSES - 1),
             )
 
-        def store_rows(out, tile, i):
-            rows = out.rearrange("(m i) n -> m i n", i=ROWS)
-            nc.sync.dma_start(out=rows[:, i : i + 2, :], in_=tile[:, i : i + 2, :])
+        def store(out, tile):
+            nc.sync.dma_start(out=out.rearrange("(m i) n -> m i n", i=ROWS), in_=tile[:])
 
         def multiply_v(acc, a, i):
             multiply(acc, a, i, wv_codes[a][:].bitcast(E4M3X4), wv_sc[a][:])
@@ -93,10 +92,9 @@ def tile_mix_qkv3_tm_none_kernel(
             nc.vector.memset(wk_sc[:].bitcast(I32), 0)
             load_pass(x_raw[0], x, 0)
             load_scales(wq_sc, wq_scales)
-            nc.sync.dma_start(out=wq_sb[:, 0, :], in_=wq_words[0])
+            nc.sync.dma_start(out=wq_sb[:], in_=wq_words.rearrange("a p n -> p a n"))
             for a in range(1, PASSES):
                 load_pass(x_raw[a], x, a)
-                nc.sync.dma_start(out=wq_sb[:, a, :], in_=wq_words[a])
             load_scales(wk_sc, wk_scales)
             nc.sync.dma_start(out=wk_sb[:], in_=wk_words.rearrange("a p m i -> p a (m i)"))
             for a in range(PASSES):
@@ -120,8 +118,7 @@ def tile_mix_qkv3_tm_none_kernel(
             for i in range(ROWS):
                 nc.vector.tensor_copy(out=q_out[:, i, :N_MM], in_=q_acc[2 * i][:])
                 nc.scalar.copy(out=q_out[:, i, N_MM:], in_=q_acc[2 * i + 1][:])
-                if i % 2 == 1:
-                    store_rows(out_0, q_out, i - 1)
+            store(out_0, q_out)
 
             k_acc = [psum.tile([P, N_MM], F32, name=f"bank{b}") for b in range(4)]
             for i in range(ROWS):
@@ -141,11 +138,11 @@ def tile_mix_qkv3_tm_none_kernel(
                 for i in range(ROWS):
                     multiply_v(v_acc[i], a, i)
                 if a < 2:
-                    nc.vector.tensor_copy(out=k_out[:, 2 * a, :], in_=k_acc[2 * a][:])
+                    nc.scalar.copy(out=k_out[:, 2 * a, :], in_=k_acc[2 * a][:])
                     nc.scalar.copy(out=k_out[:, 2 * a + 1, :], in_=k_acc[2 * a + 1][:])
-            nc.sync.dma_start(out=out_1.rearrange("(m i) n -> m i n", i=ROWS), in_=k_out[:])
+            store(out_1, k_out)
 
             for i in range(0, ROWS, 2):
                 nc.vector.tensor_copy(out=v_out[:, i, :], in_=v_acc[i][:])
                 nc.scalar.copy(out=v_out[:, i + 1, :], in_=v_acc[i + 1][:])
-                store_rows(out_2, v_out, i)
+            store(out_2, v_out)

@@ -42,7 +42,7 @@ def tile_mix_qkv3_tm_none_kernel(
         wq_sb = sb.tile([P, PASSES, 2 * Q], U8, name="wq_sb", align_bytes=64)
         wk_sb = sb.tile([P, PASSES, PACK * V], U8, name="wk_sb", align_bytes=64)
         wq_sc = sb.tile([P, PASSES, Q], U8, name="wq_sc", align_bytes=64)
-        wk_sc = sb.tile([P, PASSES, V], U8, name="wk_sc", align_bytes=64)
+        wk_sc = sb.tile([P, V], U8, name="wk_sc", align_bytes=64)
         q_out = sb.tile([P, ROWS, Q], F32, name="q_out", align_bytes=64)
         k_out = sb.tile([P, ROWS, V], F32, name="k_out", align_bytes=64)
         v_out = sb.tile([P, ROWS, V], F32, name="v_out", align_bytes=64)
@@ -55,6 +55,12 @@ def tile_mix_qkv3_tm_none_kernel(
             words = src.bitcast(I32).rearrange("a (q r) n -> r q a n", r=4)
             for r in range(4):
                 nc.sync.dma_start(out=dst[r:P:32, :, :].bitcast(I32), in_=words[r])
+
+        def load_packed_scales(dst, src):
+            words = src.bitcast(I32)
+            for q in range(4):
+                rows = slice(32 * q + 4, 32 * q + 4 + 4 * PASSES)
+                nc.sync.dma_start(out=dst[rows, :].bitcast(I32), in_=words[:, 4 * q : 4 * q + 4, :])
 
         def cast_x(a):
             dst = x_grp[a][:].rearrange("p i m j -> p m j i")
@@ -84,6 +90,10 @@ def tile_mix_qkv3_tm_none_kernel(
         def store(out, tile):
             nc.sync.dma_start(out=out.rearrange("(m i) n -> m i n", i=ROWS), in_=tile[:])
 
+        def store_pair(out, tile, i):
+            rows = out.rearrange("(m i) n -> m i n", i=ROWS)
+            nc.sync.dma_start(out=rows[:, i : i + 2, :], in_=tile[:, i : i + 2, :])
+
         def multiply_v(acc, a, i):
             multiply(acc, a, i, wv_codes[a][:].bitcast(E4M3X4), wv_sc[a][:])
 
@@ -95,7 +105,7 @@ def tile_mix_qkv3_tm_none_kernel(
             nc.sync.dma_start(out=wq_sb[:], in_=wq_words.rearrange("a p n -> p a n"))
             for a in range(1, PASSES):
                 load_pass(x_raw[a], x, a)
-            load_scales(wk_sc, wk_scales)
+            load_packed_scales(wk_sc, wk_scales)
             nc.sync.dma_start(out=wk_sb[:], in_=wk_words.rearrange("a p m i -> p a (m i)"))
             for a in range(PASSES):
                 load_pass(wv_raw[a], wv, a)
@@ -123,7 +133,7 @@ def tile_mix_qkv3_tm_none_kernel(
             k_acc = [psum.tile([P, N_MM], F32, name=f"bank{b}") for b in range(4)]
             for i in range(ROWS):
                 for a in range(PASSES):
-                    multiply(k_acc[i], a, i, wk_sb[:, a, :].bitcast(E4M3X4), wk_sc[:, a, :])
+                    multiply(k_acc[i], a, i, wk_sb[:, a, :].bitcast(E4M3X4), wk_sc[4 * (a + 1) :, :])
 
             def quantize_wv(a):
                 nc.vector.quantize_mx(
@@ -145,4 +155,4 @@ def tile_mix_qkv3_tm_none_kernel(
             for i in range(0, ROWS, 2):
                 nc.vector.tensor_copy(out=v_out[:, i, :], in_=v_acc[i][:])
                 nc.scalar.copy(out=v_out[:, i + 1, :], in_=v_acc[i + 1][:])
-            store(out_2, v_out)
+                store_pair(out_2, v_out, i)

@@ -39,7 +39,7 @@ def tile_mix_qkv3_tm_none_kernel(
         x_sc = [sb.tile([P, T], U8, name=f"x_sc{a}", align_bytes=64) for a in range(PASSES)]
         wv_codes = [sb.tile([P, V], U32, name=f"wv_codes{a}", align_bytes=64) for a in range(PASSES)]
         wv_sc = [sb.tile([P, V], U8, name=f"wv_sc{a}", align_bytes=64) for a in range(PASSES)]
-        wq_sb = sb.tile([P, PASSES, 2 * Q], U8, name="wq_sb", align_bytes=64)
+        wq_pass = [sb.tile([P, 2 * Q], U8, name=f"wq_pass{a}", align_bytes=64) for a in range(PASSES)]
         wk_sb = sb.tile([P, PASSES, PACK * V], U8, name="wk_sb", align_bytes=64)
         wq_sc = sb.tile([P, PASSES, Q], U8, name="wq_sc", align_bytes=64)
         wk_sc = sb.tile([P, V], U8, name="wk_sc", align_bytes=64)
@@ -54,11 +54,11 @@ def tile_mix_qkv3_tm_none_kernel(
         def load_scales(dst, src):
             words = src.bitcast(I32).rearrange("a (q r) n -> r q a n", r=4)
             for r in range(4):
-                nc.sync.dma_start(out=dst[r:P:32, :, :].bitcast(I32), in_=words[r])
+                nc.scalar.dma_start(out=dst[r:P:32, :, :].bitcast(I32), in_=words[r])
 
-        def load_packed_scales(dst, src):
+        def load_packed_scales(dst, src, quadrants):
             words = src.bitcast(I32)
-            for q in range(4):
+            for q in quadrants:
                 rows = slice(32 * q + 4, 32 * q + 4 + 4 * PASSES)
                 nc.sync.dma_start(out=dst[rows, :].bitcast(I32), in_=words[:, 4 * q : 4 * q + 4, :])
 
@@ -101,12 +101,15 @@ def tile_mix_qkv3_tm_none_kernel(
             nc.vector.memset(wq_sc[:].bitcast(I32), 0)
             nc.vector.memset(wk_sc[:].bitcast(I32), 0)
             load_pass(x_raw[0], x, 0)
+            nc.sync.dma_start(out=wq_pass[0][:], in_=wq_words[0])
+            load_pass(x_raw[1], x, 1)
             load_scales(wq_sc, wq_scales)
-            nc.sync.dma_start(out=wq_sb[:], in_=wq_words.rearrange("a p n -> p a n"))
-            for a in range(1, PASSES):
-                load_pass(x_raw[a], x, a)
-            load_packed_scales(wk_sc, wk_scales)
+            load_packed_scales(wk_sc, wk_scales, range(1))
+            nc.sync.dma_start(out=wq_pass[1][:], in_=wq_words[1])
+            load_pass(x_raw[2], x, 2)
+            nc.sync.dma_start(out=wq_pass[2][:], in_=wq_words[2])
             nc.sync.dma_start(out=wk_sb[:], in_=wk_words.rearrange("a p m i -> p a (m i)"))
+            load_packed_scales(wk_sc, wk_scales, range(1, 4))
             for a in range(PASSES):
                 load_pass(wv_raw[a], wv, a)
 
@@ -122,7 +125,7 @@ def tile_mix_qkv3_tm_none_kernel(
                         n = slice(h * N_MM, (h + 1) * N_MM)
                         multiply(
                             q_acc[2 * i + h], a, i,
-                            wq_sb[:, a, 2 * h * N_MM : 2 * (h + 1) * N_MM].bitcast(E2M1X4),
+                            wq_pass[a][:, 2 * h * N_MM : 2 * (h + 1) * N_MM].bitcast(E2M1X4),
                             wq_sc[:, a, n],
                         )
             for i in range(ROWS):

@@ -56,18 +56,21 @@ def tile_mix_qkv3_tm_none_kernel(
             for r in range(4):
                 nc.scalar.dma_start(out=dst[r:P:32, :, :].bitcast(I32), in_=words[r])
 
-        def load_packed_scales(dst, src, quadrants):
+        def load_packed_scales(dst, src):
             words = src.bitcast(I32)
-            for q in quadrants:
+            for q in range(4):
                 rows = slice(32 * q + 4, 32 * q + 4 + 4 * PASSES)
-                nc.sync.dma_start(out=dst[rows, :].bitcast(I32), in_=words[:, 4 * q : 4 * q + 4, :])
+                nc.scalar.dma_start(out=dst[rows, :].bitcast(I32), in_=words[:, 4 * q : 4 * q + 4, :])
 
         def cast_x(a):
             dst = x_grp[a][:].rearrange("p i m j -> p m j i")
             src = x_raw[a][:].rearrange("p j (m i) -> p m j i", i=ROWS)
-            s = CAST_SPLIT // ROWS
-            nc.vector.tensor_copy(out=dst[:, :s], in_=src[:, :s])
-            nc.scalar.copy(out=dst[:, s:], in_=src[:, s:])
+            if a < PASSES - 1:
+                nc.vector.tensor_copy(out=dst, in_=src)
+            else:
+                s = CAST_SPLIT // ROWS
+                nc.vector.tensor_copy(out=dst[:, :s], in_=src[:, :s])
+                nc.scalar.copy(out=dst[:, s:], in_=src[:, s:])
 
         def cast_wv(a):
             dst = wv_grp[a][:].rearrange("p (c i) j -> p c j i", i=4)
@@ -104,12 +107,11 @@ def tile_mix_qkv3_tm_none_kernel(
             nc.sync.dma_start(out=wq_pass[0][:], in_=wq_words[0])
             load_pass(x_raw[1], x, 1)
             load_scales(wq_sc, wq_scales)
-            load_packed_scales(wk_sc, wk_scales, range(1))
+            load_packed_scales(wk_sc, wk_scales)
             nc.sync.dma_start(out=wq_pass[1][:], in_=wq_words[1])
             load_pass(x_raw[2], x, 2)
             nc.sync.dma_start(out=wq_pass[2][:], in_=wq_words[2])
             nc.sync.dma_start(out=wk_sb[:], in_=wk_words.rearrange("a p m i -> p a (m i)"))
-            load_packed_scales(wk_sc, wk_scales, range(1, 4))
             for a in range(PASSES):
                 load_pass(wv_raw[a], wv, a)
 

@@ -21,6 +21,7 @@ ROWS = T // P
 N_MM = 512
 
 CAST_SPLIT = 352
+WK_PLANE = 4
 
 
 def tile_mix_qkv3_tm_none_kernel(
@@ -42,7 +43,7 @@ def tile_mix_qkv3_tm_none_kernel(
         wq_pass = [sb.tile([P, 2 * Q], U8, name=f"wq_pass{a}", align_bytes=64) for a in range(PASSES)]
         wk_sb = sb.tile([P, PASSES, PACK * V], U8, name="wk_sb", align_bytes=64)
         wq_sc = sb.tile([P, PASSES, Q], U8, name="wq_sc", align_bytes=64)
-        wk_sc = sb.tile([P, V], U8, name="wk_sc", align_bytes=64)
+        wk_sc = sb.tile([P, PASSES, V], U8, name="wk_sc", align_bytes=64)
         q_out = sb.tile([P, ROWS, Q], F32, name="q_out", align_bytes=64)
         k_out = sb.tile([P, ROWS, V], F32, name="k_out", align_bytes=64)
         v_out = sb.tile([P, ROWS, V], F32, name="v_out", align_bytes=64)
@@ -51,16 +52,10 @@ def tile_mix_qkv3_tm_none_kernel(
             rows = src[a * K_PASS : (a + 1) * K_PASS, :]
             nc.sync.dma_start(out=dst[:], in_=rows.rearrange("(p j) w -> p j w", j=PACK))
 
-        def load_scales(dst, src):
+        def load_scales(dst, src, plane):
             words = src.bitcast(I32).rearrange("a (q r) n -> r q a n", r=4)
             for r in range(4):
-                nc.scalar.dma_start(out=dst[r:P:32, :, :].bitcast(I32), in_=words[r])
-
-        def load_packed_scales(dst, src):
-            words = src.bitcast(I32)
-            for q in range(4):
-                rows = slice(32 * q + 4, 32 * q + 4 + 4 * PASSES)
-                nc.scalar.dma_start(out=dst[rows, :].bitcast(I32), in_=words[:, 4 * q : 4 * q + 4, :])
+                nc.scalar.dma_start(out=dst[plane + r : P : 32, :, :].bitcast(I32), in_=words[r])
 
         def cast_x(a):
             dst = x_grp[a][:].rearrange("p i m j -> p m j i")
@@ -106,8 +101,8 @@ def tile_mix_qkv3_tm_none_kernel(
             load_pass(x_raw[0], x, 0)
             nc.sync.dma_start(out=wq_pass[0][:], in_=wq_words[0])
             load_pass(x_raw[1], x, 1)
-            load_scales(wq_sc, wq_scales)
-            load_packed_scales(wk_sc, wk_scales)
+            load_scales(wq_sc, wq_scales, 0)
+            load_scales(wk_sc, wk_scales, WK_PLANE)
             nc.sync.dma_start(out=wq_pass[1][:], in_=wq_words[1])
             load_pass(x_raw[2], x, 2)
             nc.sync.dma_start(out=wq_pass[2][:], in_=wq_words[2])
@@ -138,7 +133,7 @@ def tile_mix_qkv3_tm_none_kernel(
             k_acc = [psum.tile([P, N_MM], F32, name=f"bank{b}") for b in range(4)]
             for i in range(ROWS):
                 for a in range(PASSES):
-                    multiply(k_acc[i], a, i, wk_sb[:, a, :].bitcast(E4M3X4), wk_sc[4 * (a + 1) :, :])
+                    multiply(k_acc[i], a, i, wk_sb[:, a, :].bitcast(E4M3X4), wk_sc[WK_PLANE:, a, :])
 
             def quantize_wv(a):
                 nc.vector.quantize_mx(

@@ -17,8 +17,10 @@ P = 128
 PACK = 4
 K_PASS = P * PACK
 PASSES = K // K_PASS
+LAST = PASSES - 1
 ROWS = T // P
 N_MM = 512
+HALF = V // 2
 
 CAST_SPLIT = 352
 WK_PLANE = 4
@@ -32,25 +34,31 @@ def tile_mix_qkv3_tm_none_kernel(
         sb = ctx.enter_context(tc.tile_pool(name="sb", bufs=1))
         psum = ctx.enter_context(tc.psum_pool(name="psum", bufs=1))
 
-        x_raw = [sb.tile([P, PACK, T], F32, name=f"x_raw{a}", align_bytes=64) for a in range(PASSES)]
-        wv_raw = [sb.tile([P, PACK, V], F32, name=f"wv_raw{a}", align_bytes=64) for a in range(PASSES)]
-        x_grp = [sb.tile([P, ROWS, P, PACK], BF16, name=f"x_grp{a}", align_bytes=64) for a in range(PASSES)]
-        wv_grp = [sb.tile([P, V, PACK], BF16, name=f"wv_grp{a}", align_bytes=64) for a in range(PASSES)]
-        x_codes = [sb.tile([P, T], U32, name=f"x_codes{a}", align_bytes=64) for a in range(PASSES)]
-        x_sc = [sb.tile([P, T], U8, name=f"x_sc{a}", align_bytes=64) for a in range(PASSES)]
-        wv_codes = [sb.tile([P, V], U32, name=f"wv_codes{a}", align_bytes=64) for a in range(PASSES)]
-        wv_sc = [sb.tile([P, V], U8, name=f"wv_sc{a}", align_bytes=64) for a in range(PASSES)]
-        wq_pass = [sb.tile([P, 2 * Q], U8, name=f"wq_pass{a}", align_bytes=64) for a in range(PASSES)]
-        wk_sb = sb.tile([P, PASSES, PACK * V], U8, name="wk_sb", align_bytes=64)
+        def per_pass(name, shape, dtype):
+            return [sb.tile(shape, dtype, name=f"{name}{a}", align_bytes=64) for a in range(PASSES)]
+
+        x_raw = per_pass("x_raw", [P, PACK, T], F32)
+        wv_raw = per_pass("wv_raw", [P, PACK, V], F32)
+        x_grp = per_pass("x_grp", [P, ROWS, P, PACK], BF16)
+        wv_grp = per_pass("wv_grp", [P, V, PACK], BF16)
+        x_codes = per_pass("x_codes", [P, T], U32)
+        x_sc = per_pass("x_sc", [P, T], U8)
+        wv_codes = per_pass("wv_codes", [P, V], U32)
+        wv_sc = per_pass("wv_sc", [P, V], U8)
+        wq_codes = per_pass("wq_codes", [P, 2 * Q], U8)
+        wk_codes = sb.tile([P, PASSES, PACK * V], U8, name="wk_codes", align_bytes=64)
         wq_sc = sb.tile([P, PASSES, Q], U8, name="wq_sc", align_bytes=64)
         wk_sc = sb.tile([P, PASSES, V], U8, name="wk_sc", align_bytes=64)
         q_out = sb.tile([P, ROWS, Q], F32, name="q_out", align_bytes=64)
         k_out = sb.tile([P, ROWS, V], F32, name="k_out", align_bytes=64)
         v_out = sb.tile([P, ROWS, V], F32, name="v_out", align_bytes=64)
 
-        def load_pass(dst, src, a):
+        def load_floats(dst, src, a):
             rows = src[a * K_PASS : (a + 1) * K_PASS, :]
-            nc.sync.dma_start(out=dst[:], in_=rows.rearrange("(p j) w -> p j w", j=PACK))
+            nc.sync.dma_start(out=dst[a][:], in_=rows.rearrange("(p j) w -> p j w", j=PACK))
+
+        def load_wq(a):
+            nc.sync.dma_start(out=wq_codes[a][:], in_=wq_words[a])
 
         def load_scales(dst, src, plane):
             words = src.bitcast(I32).rearrange("a (q r) n -> r q a n", r=4)
@@ -60,99 +68,96 @@ def tile_mix_qkv3_tm_none_kernel(
         def cast_x(a):
             dst = x_grp[a][:].rearrange("p i m j -> p m j i")
             src = x_raw[a][:].rearrange("p j (m i) -> p m j i", i=ROWS)
-            if a < PASSES - 1:
+            if a < LAST:
                 nc.vector.tensor_copy(out=dst, in_=src)
             else:
                 s = CAST_SPLIT // ROWS
                 nc.vector.tensor_copy(out=dst[:, :s], in_=src[:, :s])
                 nc.scalar.copy(out=dst[:, s:], in_=src[:, s:])
 
-        def cast_wv(a):
+        def quantize_x(a):
+            nc.vector.quantize_mx(
+                out=x_codes[a][:].bitcast(E4M3X4), scales=x_sc[a][:],
+                in_=x_grp[a][:].rearrange("p i m j -> p (i m j)"),
+            )
+
+        def prepare_wv(a, split):
             dst = wv_grp[a][:].rearrange("p (c i) j -> p c j i", i=4)
             src = wv_raw[a][:].rearrange("p j (c i) -> p c j i", i=4)
-            s = CAST_SPLIT // 4
-            nc.vector.tensor_copy(out=dst[:, :s], in_=src[:, :s])
-            nc.scalar.copy(out=dst[:, s:], in_=src[:, s:])
-
-        def x_operand(a, i):
-            cols = slice(i * P, (i + 1) * P)
-            return x_codes[a][:, cols].bitcast(E4M3X4), x_sc[a][:, cols]
+            h, s = HALF // 4, split // 4
+            nc.vector.tensor_copy(out=dst[:, :h], in_=src[:, :h])
+            nc.vector.tensor_copy(out=dst[:, h:s], in_=src[:, h:s])
+            if split < V:
+                nc.scalar.copy(out=dst[:, s:], in_=src[:, s:])
+            for cols in (slice(0, HALF), slice(HALF, V)):
+                nc.vector.quantize_mx(
+                    out=wv_codes[a][:, cols].bitcast(E4M3X4), scales=wv_sc[a][:, cols],
+                    in_=wv_grp[a][:, cols, :].rearrange("p w j -> p (w j)"),
+                )
 
         def multiply(acc, a, i, rhs, rhs_scale):
-            lhsT, lhsT_scale = x_operand(a, i)
+            cols = slice(i * P, (i + 1) * P)
             nc.tensor.matmul_mx(
-                out=acc[:], lhsT=lhsT, lhsT_scale=lhsT_scale, rhs=rhs, rhs_scale=rhs_scale,
-                start=(a == 0), stop=(a == PASSES - 1),
+                out=acc[:], lhsT=x_codes[a][:, cols].bitcast(E4M3X4), lhsT_scale=x_sc[a][:, cols],
+                rhs=rhs, rhs_scale=rhs_scale, start=(a == 0), stop=(a == LAST),
             )
+
+        def v_pass(acc, a):
+            for i in range(ROWS):
+                multiply(acc[i], a, i, wv_codes[a][:].bitcast(E4M3X4), wv_sc[a][:])
+
+        def copy_out(on_vector, dst, bank):
+            if on_vector:
+                nc.vector.tensor_copy(out=dst, in_=bank[:])
+            else:
+                nc.scalar.copy(out=dst, in_=bank[:])
 
         def store(out, tile):
             nc.sync.dma_start(out=out.rearrange("(m i) n -> m i n", i=ROWS), in_=tile[:])
 
-        def store_pair(out, tile, i):
-            rows = out.rearrange("(m i) n -> m i n", i=ROWS)
-            nc.sync.dma_start(out=rows[:, i : i + 2, :], in_=tile[:, i : i + 2, :])
-
-        def multiply_v(acc, a, i):
-            multiply(acc, a, i, wv_codes[a][:].bitcast(E4M3X4), wv_sc[a][:])
-
         with tc.manual_schedule():
             nc.vector.memset(wq_sc[:].bitcast(I32), 0)
             nc.vector.memset(wk_sc[:].bitcast(I32), 0)
-            load_pass(x_raw[0], x, 0)
-            nc.sync.dma_start(out=wq_pass[0][:], in_=wq_words[0])
-            load_pass(x_raw[1], x, 1)
+            load_floats(x_raw, x, 0)
+            load_wq(0)
+            load_floats(x_raw, x, 1)
             load_scales(wq_sc, wq_scales, 0)
             load_scales(wk_sc, wk_scales, WK_PLANE)
-            nc.sync.dma_start(out=wq_pass[1][:], in_=wq_words[1])
-            load_pass(x_raw[2], x, 2)
-            nc.sync.dma_start(out=wq_pass[2][:], in_=wq_words[2])
-            nc.sync.dma_start(out=wk_sb[:], in_=wk_words.rearrange("a p m i -> p a (m i)"))
+            load_wq(1)
+            load_floats(x_raw, x, 2)
+            load_wq(2)
+            nc.sync.dma_start(out=wk_codes[:], in_=wk_words.rearrange("a p m i -> p a (m i)"))
             for a in range(PASSES):
-                load_pass(wv_raw[a], wv, a)
+                load_floats(wv_raw, wv, a)
 
             q_acc = [psum.tile([P, N_MM], F32, name=f"bank{b}") for b in range(8)]
             for a in range(PASSES):
                 cast_x(a)
-                nc.vector.quantize_mx(
-                    out=x_codes[a][:].bitcast(E4M3X4), scales=x_sc[a][:],
-                    in_=x_grp[a][:].rearrange("p i m j -> p (i m j)"),
-                )
+                quantize_x(a)
                 for i in range(ROWS):
                     for h in range(2):
-                        n = slice(h * N_MM, (h + 1) * N_MM)
                         multiply(
                             q_acc[2 * i + h], a, i,
-                            wq_pass[a][:, 2 * h * N_MM : 2 * (h + 1) * N_MM].bitcast(E2M1X4),
-                            wq_sc[:, a, n],
+                            wq_codes[a][:, 2 * h * N_MM : 2 * (h + 1) * N_MM].bitcast(E2M1X4),
+                            wq_sc[:, a, h * N_MM : (h + 1) * N_MM],
                         )
-            for i in range(ROWS):
-                nc.vector.tensor_copy(out=q_out[:, i, :N_MM], in_=q_acc[2 * i][:])
-                nc.scalar.copy(out=q_out[:, i, N_MM:], in_=q_acc[2 * i + 1][:])
+            for b in range(8):
+                i, h = divmod(b, 2)
+                copy_out(b in (0, 2, 4), q_out[:, i, h * N_MM : (h + 1) * N_MM], q_acc[b])
             store(out_0, q_out)
 
             k_acc = [psum.tile([P, N_MM], F32, name=f"bank{b}") for b in range(4)]
+            v_acc = [psum.tile([P, N_MM], F32, name=f"bank{b}") for b in range(4, 8)]
             for i in range(ROWS):
                 for a in range(PASSES):
-                    multiply(k_acc[i], a, i, wk_sb[:, a, :].bitcast(E4M3X4), wk_sc[WK_PLANE:, a, :])
-
-            def quantize_wv(a):
-                nc.vector.quantize_mx(
-                    out=wv_codes[a][:].bitcast(E4M3X4), scales=wv_sc[a][:],
-                    in_=wv_grp[a][:].rearrange("p w j -> p (w j)"),
-                )
-
-            v_acc = [psum.tile([P, N_MM], F32, name=f"bank{b}") for b in range(4, 8)]
+                    multiply(k_acc[i], a, i, wk_codes[:, a, :].bitcast(E4M3X4), wk_sc[WK_PLANE:, a, :])
             for a in range(PASSES):
-                cast_wv(a)
-                quantize_wv(a)
-                for i in range(ROWS):
-                    multiply_v(v_acc[i], a, i)
-                if a < 2:
-                    nc.scalar.copy(out=k_out[:, 2 * a, :], in_=k_acc[2 * a][:])
-                    nc.scalar.copy(out=k_out[:, 2 * a + 1, :], in_=k_acc[2 * a + 1][:])
+                prepare_wv(a, V if a == 0 else CAST_SPLIT)
+                v_pass(v_acc, a)
+                if a < LAST:
+                    for i in (2 * a, 2 * a + 1):
+                        copy_out(False, k_out[:, i, :], k_acc[i])
             store(out_1, k_out)
-
-            for i in range(0, ROWS, 2):
-                nc.vector.tensor_copy(out=v_out[:, i, :], in_=v_acc[i][:])
-                nc.scalar.copy(out=v_out[:, i + 1, :], in_=v_acc[i + 1][:])
-                store_pair(out_2, v_out, i)
+            for i in range(ROWS):
+                copy_out(i % 2 == 0, v_out[:, i, :], v_acc[i])
+            store(out_2, v_out)

@@ -35,7 +35,7 @@ def tile_mix_qkv3_tm_none_kernel(
         psum = ctx.enter_context(tc.psum_pool(name="psum", bufs=1))
 
         def per_pass(name, shape, dtype):
-            return [sb.tile(shape, dtype, name=f"{name}{a}", align_bytes=64) for a in range(PASSES)]
+            return [sb.tile(shape, dtype, name=f"{name}{a}", align_bytes=256) for a in range(PASSES)]
 
         x_raw = per_pass("x_raw", [P, PACK, T], F32)
         wv_raw = per_pass("wv_raw", [P, PACK, V], F32)
@@ -46,12 +46,12 @@ def tile_mix_qkv3_tm_none_kernel(
         wv_codes = per_pass("wv_codes", [P, V], U32)
         wv_sc = per_pass("wv_sc", [P, V], U8)
         wq_codes = per_pass("wq_codes", [P, 2 * Q], U8)
-        wk_codes = sb.tile([P, PASSES, PACK * V], U8, name="wk_codes", align_bytes=64)
-        wq_sc = sb.tile([P, PASSES, Q], U8, name="wq_sc", align_bytes=64)
-        wk_sc = sb.tile([P, PASSES, V], U8, name="wk_sc", align_bytes=64)
-        q_out = sb.tile([P, ROWS, Q], F32, name="q_out", align_bytes=64)
-        k_out = sb.tile([P, ROWS, V], F32, name="k_out", align_bytes=64)
-        v_out = sb.tile([P, ROWS, V], F32, name="v_out", align_bytes=64)
+        wk_codes = sb.tile([P, PASSES, PACK * V], U8, name="wk_codes", align_bytes=256)
+        wq_sc = sb.tile([P, PASSES, Q], U8, name="wq_sc", align_bytes=256)
+        wk_sc = sb.tile([P, PASSES, V], U8, name="wk_sc", align_bytes=256)
+        q_out = sb.tile([P, ROWS, Q], F32, name="q_out", align_bytes=256)
+        k_out = sb.tile([P, ROWS, V], F32, name="k_out", align_bytes=256)
+        v_out = sb.tile([P, ROWS, V], F32, name="v_out", align_bytes=256)
 
         def load_floats(dst, src, a):
             rows = src[a * K_PASS : (a + 1) * K_PASS, :]

@@ -23,6 +23,7 @@ N_MM = 512
 HALF = V // 2
 
 CAST_SPLIT = 352
+PAIR_SPLIT = 48
 WK_PLANE = 4
 
 
@@ -65,21 +66,23 @@ def tile_mix_qkv3_tm_none_kernel(
             for r in range(4):
                 nc.scalar.dma_start(out=dst[plane + r : P : 32, :, :].bitcast(I32), in_=words[r])
 
-        def cast_x(a):
+        def prepare_x(a):
             dst = x_grp[a][:].rearrange("p i m j -> p m j i")
             src = x_raw[a][:].rearrange("p j (m i) -> p m j i", i=ROWS)
             if a < LAST:
                 nc.vector.tensor_copy(out=dst, in_=src)
+                pieces = [slice(0, ROWS)]
             else:
-                s = CAST_SPLIT // ROWS
-                nc.vector.tensor_copy(out=dst[:, :s], in_=src[:, :s])
-                nc.scalar.copy(out=dst[:, s:], in_=src[:, s:])
-
-        def quantize_x(a):
-            nc.vector.quantize_mx(
-                out=x_codes[a][:].bitcast(E4M3X4), scales=x_sc[a][:],
-                in_=x_grp[a][:].rearrange("p i m j -> p (i m j)"),
-            )
+                pieces = [slice(0, 2), slice(2, ROWS)]
+                nc.vector.tensor_copy(out=dst[:, :, :, pieces[0]], in_=src[:, :, :, pieces[0]])
+                nc.vector.tensor_copy(out=dst[:, :PAIR_SPLIT, :, pieces[1]], in_=src[:, :PAIR_SPLIT, :, pieces[1]])
+                nc.scalar.copy(out=dst[:, PAIR_SPLIT:, :, pieces[1]], in_=src[:, PAIR_SPLIT:, :, pieces[1]])
+            for tiles in pieces:
+                cols = slice(tiles.start * P, tiles.stop * P)
+                nc.vector.quantize_mx(
+                    out=x_codes[a][:, cols].bitcast(E4M3X4), scales=x_sc[a][:, cols],
+                    in_=x_grp[a][:, tiles].rearrange("p i m j -> p (i m j)"),
+                )
 
         def prepare_wv(a, split):
             dst = wv_grp[a][:].rearrange("p (c i) j -> p c j i", i=4)
@@ -132,8 +135,7 @@ def tile_mix_qkv3_tm_none_kernel(
 
             q_acc = [psum.tile([P, N_MM], F32, name=f"bank{b}") for b in range(8)]
             for a in range(PASSES):
-                cast_x(a)
-                quantize_x(a)
+                prepare_x(a)
                 for i in range(ROWS):
                     for h in range(2):
                         multiply(
@@ -143,7 +145,7 @@ def tile_mix_qkv3_tm_none_kernel(
                         )
             for b in range(8):
                 i, h = divmod(b, 2)
-                copy_out(b in (0, 2, 4), q_out[:, i, h * N_MM : (h + 1) * N_MM], q_acc[b])
+                copy_out(h == 0, q_out[:, i, h * N_MM : (h + 1) * N_MM], q_acc[b])
             store(out_0, q_out)
 
             k_acc = [psum.tile([P, N_MM], F32, name=f"bank{b}") for b in range(4)]
@@ -152,7 +154,7 @@ def tile_mix_qkv3_tm_none_kernel(
                 for a in range(PASSES):
                     multiply(k_acc[i], a, i, wk_codes[:, a, :].bitcast(E4M3X4), wk_sc[WK_PLANE:, a, :])
             for a in range(PASSES):
-                prepare_wv(a, V if a == 0 else CAST_SPLIT)
+                prepare_wv(a, CAST_SPLIT)
                 v_pass(v_acc, a)
                 if a < LAST:
                     for i in (2 * a, 2 * a + 1):

@@ -160,6 +160,8 @@ def tile_mix_qkv3_tm_none_kernel(
                     for i in (2 * a, 2 * a + 1):
                         copy_out(False, k_out[:, i, :], k_acc[i])
             store(out_1, k_out)
+            v_rows = out_2.rearrange("(m i) n -> m i n", i=ROWS)
             for i in range(ROWS):
                 copy_out(i % 2 == 0, v_out[:, i, :], v_acc[i])
-            store(out_2, v_out)
+                if i % 2 == 1:
+                    nc.sync.dma_start(out=v_rows[:, i - 1 : i + 1, :], in_=v_out[:, i - 1 : i + 1, :])

@@ -24,7 +24,6 @@ HALF = V // 2
 
 CAST_SPLIT = 352
 PAIR_SPLIT = 48
-WK_PLANE = 4
 
 
 def tile_mix_qkv3_tm_none_kernel(
@@ -49,7 +48,7 @@ def tile_mix_qkv3_tm_none_kernel(
         wq_codes = per_pass("wq_codes", [P, 2 * Q], U8)
         wk_codes = sb.tile([P, PASSES, PACK * V], U8, name="wk_codes", align_bytes=256)
         wq_sc = sb.tile([P, PASSES, Q], U8, name="wq_sc", align_bytes=256)
-        wk_sc = sb.tile([P, PASSES, V], U8, name="wk_sc", align_bytes=256)
+        wk_sc = sb.tile([P, V], U8, name="wk_sc", align_bytes=256)
         q_out = sb.tile([P, ROWS, Q], F32, name="q_out", align_bytes=256)
         k_out = sb.tile([P, ROWS, V], F32, name="k_out", align_bytes=256)
         v_out = sb.tile([P, ROWS, V], F32, name="v_out", align_bytes=256)
@@ -61,10 +60,13 @@ def tile_mix_qkv3_tm_none_kernel(
         def load_wq(a):
             nc.sync.dma_start(out=wq_codes[a][:], in_=wq_words[a])
 
-        def load_scales(dst, src, plane):
-            words = src.bitcast(I32).rearrange("a (q r) n -> r q a n", r=4)
-            for r in range(4):
-                nc.scalar.dma_start(out=dst[plane + r : P : 32, :, :].bitcast(I32), in_=words[r])
+        def load_wq_scales(r):
+            words = wq_scales.bitcast(I32).rearrange("a (q r) n -> r q a n", r=4)
+            nc.scalar.dma_start(out=wq_sc[r : P : 32, :, :].bitcast(I32), in_=words[r])
+
+        def load_wk_scales(queue, q):
+            words = wk_scales.bitcast(I32)[:, 4 * q : 4 * q + 4, :]
+            queue.dma_start(out=wk_sc[32 * q : 32 * q + 4 * PASSES, :].bitcast(I32), in_=words)
 
         def prepare_x(a):
             dst = x_grp[a][:].rearrange("p i m j -> p m j i")
@@ -115,17 +117,21 @@ def tile_mix_qkv3_tm_none_kernel(
             else:
                 nc.scalar.copy(out=dst, in_=bank[:])
 
-        def store(out, tile):
-            nc.sync.dma_start(out=out.rearrange("(m i) n -> m i n", i=ROWS), in_=tile[:])
+        def store(out, tile, tiles):
+            rows = out.rearrange("(m i) n -> m i n", i=ROWS)
+            nc.sync.dma_start(out=rows[:, tiles, :], in_=tile[:, tiles, :])
 
         with tc.manual_schedule():
-            nc.vector.memset(wq_sc[:].bitcast(I32), 0)
             nc.vector.memset(wk_sc[:].bitcast(I32), 0)
+            nc.vector.memset(wq_sc[:].bitcast(I32), 0)
             load_floats(x_raw, x, 0)
+            load_wk_scales(nc.sync, 3)
             load_wq(0)
+            for r in range(4):
+                load_wq_scales(r)
             load_floats(x_raw, x, 1)
-            load_scales(wq_sc, wq_scales, 0)
-            load_scales(wk_sc, wk_scales, WK_PLANE)
+            for q in range(3):
+                load_wk_scales(nc.scalar, q)
             load_wq(1)
             load_floats(x_raw, x, 2)
             load_wq(2)
@@ -146,22 +152,21 @@ def tile_mix_qkv3_tm_none_kernel(
             for b in range(8):
                 i, h = divmod(b, 2)
                 copy_out(h == 0, q_out[:, i, h * N_MM : (h + 1) * N_MM], q_acc[b])
-            store(out_0, q_out)
+            store(out_0, q_out, slice(0, ROWS))
 
             k_acc = [psum.tile([P, N_MM], F32, name=f"bank{b}") for b in range(4)]
             v_acc = [psum.tile([P, N_MM], F32, name=f"bank{b}") for b in range(4, 8)]
             for i in range(ROWS):
                 for a in range(PASSES):
-                    multiply(k_acc[i], a, i, wk_codes[:, a, :].bitcast(E4M3X4), wk_sc[WK_PLANE:, a, :])
+                    multiply(k_acc[i], a, i, wk_codes[:, a, :].bitcast(E4M3X4), wk_sc[4 * a :, :])
             for a in range(PASSES):
                 prepare_wv(a, CAST_SPLIT)
                 v_pass(v_acc, a)
                 if a < LAST:
                     for i in (2 * a, 2 * a + 1):
                         copy_out(False, k_out[:, i, :], k_acc[i])
-            store(out_1, k_out)
-            v_rows = out_2.rearrange("(m i) n -> m i n", i=ROWS)
+            store(out_1, k_out, slice(0, ROWS))
             for i in range(ROWS):
                 copy_out(i % 2 == 0, v_out[:, i, :], v_acc[i])
                 if i % 2 == 1:
-                    nc.sync.dma_start(out=v_rows[:, i - 1 : i + 1, :], in_=v_out[:, i - 1 : i + 1, :])
+                    store(out_2, v_out, slice(i - 1, i + 1))

@@ -45,10 +45,12 @@ def tile_mix_qkv3_tm_none_kernel(
         x_sc = per_pass("x_sc", [P, T], U8)
         wv_codes = per_pass("wv_codes", [P, V], U32)
         wv_sc = per_pass("wv_sc", [P, V], U8)
-        wq_codes = per_pass("wq_codes", [P, 2 * Q], U8)
+        wq_first = sb.tile([P, 2 * Q], U8, name="wq_first", align_bytes=256)
+        wq_rest = sb.tile([P, LAST, 2 * Q], U8, name="wq_rest", align_bytes=256)
+        wq_codes = [wq_first[:]] + [wq_rest[:, a, :] for a in range(LAST)]
         wk_codes = sb.tile([P, PASSES, PACK * V], U8, name="wk_codes", align_bytes=256)
         wq_sc = sb.tile([P, PASSES, Q], U8, name="wq_sc", align_bytes=256)
-        wk_sc = sb.tile([P, V], U8, name="wk_sc", align_bytes=256)
+        wk_sc = sb.tile([P, PASSES, V], U8, name="wk_sc", align_bytes=256)
         q_out = sb.tile([P, ROWS, Q], F32, name="q_out", align_bytes=256)
         k_out = sb.tile([P, ROWS, V], F32, name="k_out", align_bytes=256)
         v_out = sb.tile([P, ROWS, V], F32, name="v_out", align_bytes=256)
@@ -57,16 +59,13 @@ def tile_mix_qkv3_tm_none_kernel(
             rows = src[a * K_PASS : (a + 1) * K_PASS, :]
             nc.sync.dma_start(out=dst[a][:], in_=rows.rearrange("(p j) w -> p j w", j=PACK))
 
-        def load_wq(a):
-            nc.sync.dma_start(out=wq_codes[a][:], in_=wq_words[a])
-
         def load_wq_scales(r):
             words = wq_scales.bitcast(I32).rearrange("a (q r) n -> r q a n", r=4)
             nc.scalar.dma_start(out=wq_sc[r : P : 32, :, :].bitcast(I32), in_=words[r])
 
-        def load_wk_scales(queue, q):
-            words = wk_scales.bitcast(I32)[:, 4 * q : 4 * q + 4, :]
-            queue.dma_start(out=wk_sc[32 * q : 32 * q + 4 * PASSES, :].bitcast(I32), in_=words)
+        def load_wk_scales(queue, r):
+            words = wk_scales.bitcast(I32).rearrange("a (q r) n -> r q a n", r=4)
+            queue.dma_start(out=wk_sc[4 + r : P : 32, :, :].bitcast(I32), in_=words[r])
 
         def prepare_x(a):
             dst = x_grp[a][:].rearrange("p i m j -> p m j i")
@@ -122,19 +121,18 @@ def tile_mix_qkv3_tm_none_kernel(
             nc.sync.dma_start(out=rows[:, tiles, :], in_=tile[:, tiles, :])
 
         with tc.manual_schedule():
-            nc.vector.memset(wk_sc[:].bitcast(I32), 0)
             nc.vector.memset(wq_sc[:].bitcast(I32), 0)
+            nc.vector.memset(wk_sc[:].bitcast(I32), 0)
             load_floats(x_raw, x, 0)
             load_wk_scales(nc.sync, 3)
-            load_wq(0)
+            nc.sync.dma_start(out=wq_first[:], in_=wq_words[0])
             for r in range(4):
                 load_wq_scales(r)
             load_floats(x_raw, x, 1)
             for q in range(3):
                 load_wk_scales(nc.scalar, q)
-            load_wq(1)
+            nc.sync.dma_start(out=wq_rest[:], in_=wq_words[1:].rearrange("a p n -> p a n"))
             load_floats(x_raw, x, 2)
-            load_wq(2)
             nc.sync.dma_start(out=wk_codes[:], in_=wk_words.rearrange("a p m i -> p a (m i)"))
             for a in range(PASSES):
                 load_floats(wv_raw, wv, a)
@@ -158,7 +156,7 @@ def tile_mix_qkv3_tm_none_kernel(
             v_acc = [psum.tile([P, N_MM], F32, name=f"bank{b}") for b in range(4, 8)]
             for i in range(ROWS):
                 for a in range(PASSES):
-                    multiply(k_acc[i], a, i, wk_codes[:, a, :].bitcast(E4M3X4), wk_sc[4 * a :, :])
+                    multiply(k_acc[i], a, i, wk_codes[:, a, :].bitcast(E4M3X4), wk_sc[4:, a, :])
             for a in range(PASSES):
                 prepare_wv(a, CAST_SPLIT)
                 v_pass(v_acc, a)

@@ -61,7 +61,11 @@ def tile_mix_qkv3_tm_none_kernel(
 
         def load_wq_scales(r):
             words = wq_scales.bitcast(I32).rearrange("a (q r) n -> r q a n", r=4)
-            nc.scalar.dma_start(out=wq_sc[r : P : 32, :, :].bitcast(I32), in_=words[r])
+            if r == 0:
+                for q in range(2):
+                    nc.scalar.dma_start(out=wq_sc[32 * q : P : 64, :, :].bitcast(I32), in_=words[r][q::2])
+            else:
+                nc.scalar.dma_start(out=wq_sc[r : P : 32, :, :].bitcast(I32), in_=words[r])
 
         def load_wk_scales(queue, r):
             words = wk_scales.bitcast(I32).rearrange("a (q r) n -> r q a n", r=4)

from contextlib import ExitStack

import concourse.mybir as mybir

K, Q, V, T = 1536, 1024, 512, 512
FLOPS = 2 * K * T * (Q + 2 * V)

F32 = mybir.dt.float32
BF16 = mybir.dt.bfloat16
I32 = mybir.dt.int32
U32 = mybir.dt.uint32
U8 = mybir.dt.uint8
E4M3X4 = mybir.dt.float8_e4m3fn_x4
E2M1X4 = mybir.dt.float4_e2m1fn_x4

P = 128
PACK = 4
K_PASS = P * PACK
PASSES = K // K_PASS
LAST = PASSES - 1
ROWS = T // P
N_MM = 512
HALF = V // 2

CAST_SPLIT = 352
PAIR_SPLIT = 48


def tile_mix_qkv3_tm_none_kernel(
    tc, x, wq_words, wq_scales, wk_words, wk_scales, wv, out_0, out_1, out_2
):
    nc = tc.nc
    with ExitStack() as ctx:
        sb = ctx.enter_context(tc.tile_pool(name="sb", bufs=1))
        psum = ctx.enter_context(tc.psum_pool(name="psum", bufs=1))

        def per_pass(name, shape, dtype):
            return [sb.tile(shape, dtype, name=f"{name}{a}", align_bytes=256) for a in range(PASSES)]

        x_raw = per_pass("x_raw", [P, PACK, T], F32)
        wv_raw = per_pass("wv_raw", [P, PACK, V], F32)
        x_grp = per_pass("x_grp", [P, ROWS, P, PACK], BF16)
        wv_grp = per_pass("wv_grp", [P, V, PACK], BF16)
        x_codes = per_pass("x_codes", [P, T], U32)
        x_sc = per_pass("x_sc", [P, T], U8)
        wv_codes = per_pass("wv_codes", [P, V], U32)
        wv_sc = per_pass("wv_sc", [P, V], U8)
        wq_first = sb.tile([P, 2 * Q], U8, name="wq_first", align_bytes=256)
        wq_rest = sb.tile([P, LAST, 2 * Q], U8, name="wq_rest", align_bytes=256)
        wq_codes = [wq_first[:]] + [wq_rest[:, a, :] for a in range(LAST)]
        wk_codes = sb.tile([P, PASSES, PACK * V], U8, name="wk_codes", align_bytes=256)
        wq_sc = sb.tile([P, PASSES, Q], U8, name="wq_sc", align_bytes=256)
        wk_sc = sb.tile([P, PASSES, V], U8, name="wk_sc", align_bytes=256)
        q_out = sb.tile([P, ROWS, Q], F32, name="q_out", align_bytes=256)
        k_out = sb.tile([P, ROWS, V], F32, name="k_out", align_bytes=256)
        v_out = sb.tile([P, ROWS, V], F32, name="v_out", align_bytes=256)

        def load_floats(dst, src, a):
            rows = src[a * K_PASS : (a + 1) * K_PASS, :]
            nc.sync.dma_start(out=dst[a][:], in_=rows.rearrange("(p j) w -> p j w", j=PACK))

        def load_wq_scales(r):
            words = wq_scales.bitcast(I32).rearrange("a (q r) n -> r q a n", r=4)
            if r == 0:
                for q in range(2):
                    nc.scalar.dma_start(out=wq_sc[32 * q : P : 64, :, :].bitcast(I32), in_=words[r][q::2])
            else:
                nc.scalar.dma_start(out=wq_sc[r : P : 32, :, :].bitcast(I32), in_=words[r])

        def load_wk_scales(queue, r):
            words = wk_scales.bitcast(I32).rearrange("a (q r) n -> r q a n", r=4)
            queue.dma_start(out=wk_sc[4 + r : P : 32, :, :].bitcast(I32), in_=words[r])

        def prepare_x(a):
            dst = x_grp[a][:].rearrange("p i m j -> p m j i")
            src = x_raw[a][:].rearrange("p j (m i) -> p m j i", i=ROWS)
            if a < LAST:
                nc.vector.tensor_copy(out=dst, in_=src)
                pieces = [slice(0, ROWS)]
            else:
                pieces = [slice(0, 2), slice(2, ROWS)]
                nc.vector.tensor_copy(out=dst[:, :, :, pieces[0]], in_=src[:, :, :, pieces[0]])
                nc.vector.tensor_copy(out=dst[:, :PAIR_SPLIT, :, pieces[1]], in_=src[:, :PAIR_SPLIT, :, pieces[1]])
                nc.scalar.copy(out=dst[:, PAIR_SPLIT:, :, pieces[1]], in_=src[:, PAIR_SPLIT:, :, pieces[1]])
            for tiles in pieces:
                cols = slice(tiles.start * P, tiles.stop * P)
                nc.vector.quantize_mx(
                    out=x_codes[a][:, cols].bitcast(E4M3X4), scales=x_sc[a][:, cols],
                    in_=x_grp[a][:, tiles].rearrange("p i m j -> p (i m j)"),
                )

        def prepare_wv(a, split):
            dst = wv_grp[a][:].rearrange("p (c i) j -> p c j i", i=4)
            src = wv_raw[a][:].rearrange("p j (c i) -> p c j i", i=4)
            h, s = HALF // 4, split // 4
            nc.vector.tensor_copy(out=dst[:, :h], in_=src[:, :h])
            nc.vector.tensor_copy(out=dst[:, h:s], in_=src[:, h:s])
            if split < V:
                nc.scalar.copy(out=dst[:, s:], in_=src[:, s:])
            for cols in (slice(0, HALF), slice(HALF, V)):
                nc.vector.quantize_mx(
                    out=wv_codes[a][:, cols].bitcast(E4M3X4), scales=wv_sc[a][:, cols],
                    in_=wv_grp[a][:, cols, :].rearrange("p w j -> p (w j)"),
                )

        def multiply(acc, a, i, rhs, rhs_scale):
            cols = slice(i * P, (i + 1) * P)
            nc.tensor.matmul_mx(
                out=acc[:], lhsT=x_codes[a][:, cols].bitcast(E4M3X4), lhsT_scale=x_sc[a][:, cols],
                rhs=rhs, rhs_scale=rhs_scale, start=(a == 0), stop=(a == LAST),
            )

        def v_pass(acc, a):
            for i in range(ROWS):
                multiply(acc[i], a, i, wv_codes[a][:].bitcast(E4M3X4), wv_sc[a][:])

        def copy_out(on_vector, dst, bank):
            if on_vector:
                nc.vector.tensor_copy(out=dst, in_=bank[:])
            else:
                nc.scalar.copy(out=dst, in_=bank[:])

        def store(out, tile, tiles):
            rows = out.rearrange("(m i) n -> m i n", i=ROWS)
            nc.sync.dma_start(out=rows[:, tiles, :], in_=tile[:, tiles, :])

        with tc.manual_schedule():
            nc.vector.memset(wq_sc[:].bitcast(I32), 0)
            nc.vector.memset(wk_sc[:].bitcast(I32), 0)
            load_floats(x_raw, x, 0)
            load_wk_scales(nc.sync, 3)
            nc.sync.dma_start(out=wq_first[:], in_=wq_words[0])
            for r in range(4):
                load_wq_scales(r)
            load_floats(x_raw, x, 1)
            for q in range(3):
                load_wk_scales(nc.scalar, q)
            nc.sync.dma_start(out=wq_rest[:], in_=wq_words[1:].rearrange("a p n -> p a n"))
            load_floats(x_raw, x, 2)
            nc.sync.dma_start(out=wk_codes[:], in_=wk_words.rearrange("a p m i -> p a (m i)"))
            for a in range(PASSES):
                load_floats(wv_raw, wv, a)

            q_acc = [psum.tile([P, N_MM], F32, name=f"bank{b}") for b in range(8)]
            for a in range(PASSES):
                prepare_x(a)
                for i in range(ROWS):
                    for h in range(2):
                        multiply(
                            q_acc[2 * i + h], a, i,
                            wq_codes[a][:, 2 * h * N_MM : 2 * (h + 1) * N_MM].bitcast(E2M1X4),
                            wq_sc[:, a, h * N_MM : (h + 1) * N_MM],
                        )
            for b in range(8):
                i, h = divmod(b, 2)
                copy_out(h == 0, q_out[:, i, h * N_MM : (h + 1) * N_MM], q_acc[b])
            store(out_0, q_out, slice(0, ROWS))

            k_acc = [psum.tile([P, N_MM], F32, name=f"bank{b}") for b in range(4)]
            v_acc = [psum.tile([P, N_MM], F32, name=f"bank{b}") for b in range(4, 8)]
            for i in range(ROWS):
                for a in range(PASSES):
                    multiply(k_acc[i], a, i, wk_codes[:, a, :].bitcast(E4M3X4), wk_sc[4:, a, :])
            for a in range(PASSES):
                prepare_wv(a, CAST_SPLIT)
                v_pass(v_acc, a)
                if a < LAST:
                    for i in (2 * a, 2 * a + 1):
                        copy_out(False, k_out[:, i, :], k_acc[i])
            store(out_1, k_out, slice(0, ROWS))
            for i in range(ROWS):
                copy_out(i % 2 == 0, v_out[:, i, :], v_acc[i])
                if i % 2 == 1:
                    store(out_2, v_out, slice(i - 1, i + 1))
